import numpy as np
import ml_dtypes


def mxq(x, axis, fmt="e4m3"):
    dtype, down = {"e4m3": (ml_dtypes.float8_e4m3fn, 7), "e5m2": (ml_dtypes.float8_e5m2, 14)}[fmt]
    v = np.moveaxis(np.asarray(x, np.float32).astype(ml_dtypes.bfloat16).astype(np.float64), axis, -1)
    blocks = v.reshape(v.shape[:-1] + (-1, 32))
    amax = np.abs(blocks).max(-1, keepdims=True)
    byte = np.maximum(np.where(amax > 0, np.frexp(amax)[1] - 1 + 127, 0) - down, 1)
    scale = np.exp2(byte - 127.0)
    codes = (blocks / scale).astype(np.float32).astype(dtype).astype(np.float64)
    return np.moveaxis((codes * scale).reshape(v.shape), -1, axis)


WIDE = False


def mx_kscale(k):
    if not WIDE:
        return np.ones(k)
    levels = np.array([10, -10, 5, -5, 0])
    if k % 512:
        return np.exp2(np.random.permutation(np.resize(levels, k // 32))).repeat(32)
    a = np.empty((k // 512, 16))
    for p in range(k // 512):
        a[p, :8] = np.random.permutation(np.resize(levels, 8))
        for g in range(8):
            far = levels[np.abs(levels - a[p, g]) >= 10]
            a[p, g + 8] = far[np.random.randint(len(far))]
    return np.exp2(a.ravel()).repeat(32)


def f64(x):
    return np.asarray(x).astype(np.float64)


def striped(idx):
    return np.tile(idx.reshape(-1, 16).T, (8, 1)).astype(np.uint16)


def unstriped(offs):
    return offs[:16].T.reshape(-1).astype(np.int64)


def striped8(idx):
    return np.concatenate([x.reshape(-1, 16).T for x in idx]).astype(np.uint16)


def runs(offs, k):
    lists = np.stack([offs[16 * r : 16 * r + 16].T.reshape(-1) for r in range(8)]).astype(np.int64)
    return lists[np.arange(k) % 512 // 64]


def pack_weight(w):
    k, n = w.shape
    w = f64(np.asarray(w, np.float32).astype(ml_dtypes.bfloat16)).reshape(k // 32, 32, n)
    amax = np.abs(w).max(1)
    byte = np.clip(np.where(amax > 0, np.frexp(amax)[1] - 1 + 127 - 7, 1), 1, 254)
    scaled = (w * np.exp2(127.0 - byte)[:, None, :]).reshape(k, n).astype(np.float32)
    words = np.ascontiguousarray(scaled.reshape(k // 512, 128, 4, n).transpose(0, 1, 3, 2)).astype(ml_dtypes.float8_e4m3fn).view(np.uint8)
    return words, np.ascontiguousarray(byte.astype(np.uint8).reshape(k // 512, 16, n))


def unpack_weight(words, scales):
    g, p, n, _ = words.shape
    vals = np.ascontiguousarray(words).view(ml_dtypes.float8_e4m3fn).astype(np.float64) * np.repeat(np.exp2(scales.astype(np.float64) - 127.0), 8, axis=1)[..., None]
    return vals.transpose(0, 1, 3, 2).reshape(g * 512, n)


def sigmoid(v):
    return 1.0 / (1.0 + np.exp(-np.maximum(v, -700.0)))

def planes(y):
    n, m = y.shape
    v = y.astype(np.float32).astype(ml_dtypes.bfloat16).astype(np.float64).reshape(n // 32, 32, m)
    top = np.abs(v).max(1)
    byte = np.clip(np.where(top > 0, np.frexp(top)[1] - 1 + 127 - 7, 1), 1, 254)
    codes = (v * np.exp2(127.0 - byte)[:, None, :]).reshape(n, m).astype(np.float32).astype(ml_dtypes.float8_e4m3fn).view(np.uint8)
    words = codes.reshape(n // 512, 128, 4, m).transpose(0, 1, 3, 2)
    return np.ascontiguousarray(words), np.ascontiguousarray(byte.astype(np.uint8).reshape(n // 512, 16, m))


K, T, S, N, G, H, W = 512, 1024, 512, 512, 2048, 512, 256


def setup_inputs():
    n = np.random.standard_normal
    s = mx_kscale(K)[:, None]
    u = mx_kscale(S)
    packed_xT = pack_weight(n((K, T)) * s)
    packed_dT = pack_weight(n((K, G)) / s)
    packed_w1 = pack_weight(n((H, N)) / np.sqrt(H) / u[:, None])
    perm = np.random.permutation(S)
    return {
        "x_words": packed_xT[0],
        "x_scales": packed_xT[1],
        "d_words": packed_dT[0],
        "d_scales": packed_dT[1],
        "gn": (np.random.uniform(0.5, 1.5, (H, 1)) * u[:, None]).astype(np.float32),
        "w1_words": packed_w1[0],
        "w1_scales": packed_w1[1],
        "sl": np.random.uniform(1.0, 2.0, (N, 1)).astype(np.float32),
        "th": (0.5 * n((N, 1))).astype(np.float32),
        "offs": striped(np.random.permutation(T)[:S]),
        "k1": striped8(np.random.randint(0, G, (8, H))),
        "two": striped(np.random.permutation(T)[:S]),
        "k2": striped8(np.random.randint(0, G, (8, H))),
        "n1": striped8(np.stack([np.random.permutation(S) for _ in range(8)])),
        "n2": striped8(np.stack([np.random.permutation(S) for _ in range(8)])),
        "n3": striped(perm[:W]),
        "n4": striped(perm[W:]),
    }


def reference(x_words, x_scales, d_words, d_scales, gn, w1_words, w1_scales, sl, th, offs, k1, two, k2, n1, n2, n3, n4):
    d_k1 = unpack_weight(d_words, d_scales)[np.arange(K)[:, None], runs(k1, K)]
    xq = unpack_weight(x_words, x_scales)[:, unstriped(offs)]
    a = 0.0625 * (d_k1.T @ xq)
    d_k2 = unpack_weight(d_words, d_scales)[np.arange(K)[:, None], runs(k2, K)]
    x_two = unpack_weight(x_words, x_scales)[:, unstriped(two)]
    b = 0.0625 * (d_k2.T @ x_two)
    z = f64(gn) * (a + (sigmoid(b[np.arange(H)[:, None], runs(n2, H)] - b)) * (a[np.arange(H)[:, None], runs(n1, H)] - a))
    h = unpack_weight(w1_words, w1_scales).T @ mxq(z, 0, "e4m3")
    pb = h[:, unstriped(n4)]
    sg = sigmoid(f64(sl) * (h[:, unstriped(n3)] - f64(th)))
    rb = pb - sg
    pa = h[:, unstriped(n3)]
    sg2 = sigmoid(f64(sl) * (h[:, unstriped(n4)] - f64(th)))
    ra = pa * sg2
    ds = np.zeros((N, S))
    ds[:, unstriped(n3)] = ra
    out = ds.copy()
    out[:, unstriped(n4)] = rb
    return (out,) + planes(out)

@@ -1,0 +1,268 @@
+from contextlib import ExitStack
+
+import concourse.mybir as mybir
+
+F32 = mybir.dt.float32
+BF16 = mybir.dt.bfloat16
+I32 = mybir.dt.int32
+U32 = mybir.dt.uint32
+U16 = mybir.dt.uint16
+U8 = mybir.dt.uint8
+FP8X4 = mybir.dt.float8_e4m3fn_x4
+ALU = mybir.AluOpType
+ACT = mybir.ActivationFunctionType
+
+P = 128
+PACK = 4
+S = 512
+HALF = S // 2
+T, G = 1024, 2048
+ROWS = 16
+ALIGN = 64
+A_ON_VECTOR = 2
+
+FLOPS = 3 * 2 * 512 * 512 * 512
+
+
+def tile_picked_twpqpullbeod_none_po_kernel(
+    tc, x_words, x_scales, d_words, d_scales, gn, w1_words, w1_scales, sl, th,
+    offs, k1, two, k2, n1, n2, n3, n4, out_0, out_1, out_2,
+):
+    nc = tc.nc
+    with ExitStack() as ctx:
+        lists = ctx.enter_context(tc.tile_pool(name="lists", bufs=1))
+        sb = ctx.enter_context(tc.tile_pool(name="sb", bufs=1))
+        psum = ctx.enter_context(tc.psum_pool(name="psum", bufs=1))
+
+        def tile(shape, dtype, name, tag=None):
+            return sb.tile(shape, dtype, name=name, tag=tag or name, align_bytes=ALIGN)
+
+        def bank(shape, name, index):
+            return psum.tile(shape, F32, name=name, tag="bank%d" % index)
+
+        def load_list(src, name):
+            held = lists.tile(list(src.shape), U16, name=name)
+            nc.sync.dma_start(held[:], src)
+            return held
+
+        def load_words(src, name, queue, tag=None):
+            held = tile([P, src.shape[2]], U32, name, tag)
+            queue.dma_start(held[:].bitcast(I32), src[0].rearrange("p n t -> p (n t)").bitcast(I32))
+            return held
+
+        def load_scale_window(src, name):
+            width = src.shape[2]
+            held = tile([P, width], U8, name)
+            rows = src[0].bitcast(I32).unsqueeze(1).to_broadcast([ROWS, P // ROWS, width // 4])
+            nc.sync.dma_start(held[:].bitcast(I32), rows)
+            return held
+
+        def load_column(src, name):
+            held = tile([P, PACK], F32, name)
+            nc.gpsimd.dma_start(held[:], src.rearrange("(p t) o -> p (t o)", t=PACK))
+            return held
+
+        k2_l = load_list(k2, "k2_l")
+        d_bytes = load_scale_window(d_scales, "d_bytes")
+        two_l = load_list(two, "two_l")
+        x_bytes = load_scale_window(x_scales, "x_bytes")
+        k1_l = load_list(k1, "k1_l")
+        offs_l = load_list(offs, "offs_l")
+        x_table = load_words(x_words, "x_table", nc.sync)
+        d_table = load_words(d_words, "d_table", nc.sync)
+
+        gain = load_column(gn, "gain")
+        slope = load_column(sl, "slope")
+        thresh = load_column(th, "thresh")
+        gain_full = tile([P, PACK], F32, "gain_full")
+        gain_half = tile([P, PACK], F32, "gain_half")
+        gain_back = tile([P, PACK], F32, "gain_back")
+        for scaled, factor in ((gain_half, 0.03125), (gain_back, -0.03125), (gain_full, 0.0625)):
+            nc.gpsimd.tensor_scalar(scaled[:], gain[:], factor, 0.0, ALU.mult, ALU.add)
+        shift = tile([P, PACK], F32, "shift")
+        nc.gpsimd.tensor_tensor(shift[:], slope[:], thresh[:], ALU.mult)
+        bias = tile([P, PACK], F32, "bias")
+        nc.gpsimd.tensor_scalar(bias[:], shift[:], -1.0, 0.0, ALU.mult, ALU.add)
+        w_raw_bytes = tile([P, S], U8, "w_raw_bytes")
+        nc.gpsimd.memset(w_raw_bytes[:].bitcast(I32), 0)
+        for q in range(4):
+            nc.gpsimd.dma_start(w_raw_bytes[32 * q : 32 * q + 4, :].bitcast(I32), w1_scales[0, 4 * q : 4 * q + 4, :].bitcast(I32))
+
+        planes_b = tile([P, 2 * S], U8, "planes_b")
+        planes_a = tile([P, 2 * S], U8, "planes_a")
+        nc.vector.memset(planes_b[:].bitcast(I32), 0)
+        nc.vector.memset(planes_a[:].bitcast(I32), 0)
+
+        def deal_words(engine_copy, dst, src):
+            engine_copy(dst[:].rearrange("p (t c i) -> p c t i", t=PACK, i=4), src[:].rearrange("p (c i t) -> p c t i", t=PACK, i=4))
+
+        def deal_bytes(engine_copy, dst, src):
+            engine_copy(dst.rearrange("p (t m) -> p t m", t=PACK), src.rearrange("p (m t) -> p t m", t=PACK))
+
+        def pick_scales(d_list, x_list, planes, queue, name, tag):
+            picked = tile([P, 2 * S], U8, name + "_picked", tag)
+            nc.vector.tensor_copy(picked[:, :S], d_bytes[:].indirect(d_list[:]))
+            nc.vector.tensor_copy(picked[:, S:], x_bytes[:].indirect(x_list[:]))
+            dealt = tile([P, 2 * S], U8, name + "_dealt")
+            deal_bytes(nc.vector.tensor_copy, dealt[:, :S], picked[:, :S])
+            nc.vector.tensor_copy(dealt[:, S:].bitcast(I32), picked[:, S:].bitcast(I32))
+            for v in range(4):
+                queue.dma_start(planes[v:P:32, :].bitcast(I32), dealt[8 * v : P : 32, :].bitcast(I32))
+
+        def pick_words(table, which, name, tag):
+            picked = tile([P, S], U32, name, tag)
+            nc.vector.tensor_copy(picked[:], table[:].indirect(which[:]))
+            return picked
+
+        def product(dealt, moving, planes, name, first_bank):
+            banks = []
+            for t in range(PACK):
+                acc = bank([P, S], "%s%d" % (name, t), first_bank + t)
+                cols = slice(P * t, P * (t + 1))
+                nc.tensor.matmul_mx(
+                    acc[:], lhsT=dealt[:, cols].bitcast(FP8X4), lhsT_scale=planes[:, cols],
+                    rhs=moving[:].bitcast(FP8X4), rhs_scale=planes[:, S:], start=True, stop=True,
+                )
+                banks.append(acc)
+            return banks
+
+        pick_scales(k2_l, two_l, planes_b, nc.sync, "b_bytes", "b_picked")
+        n2_l = load_list(n2, "n2_l")
+        n1_l = load_list(n1, "n1_l")
+        n3_l = load_list(n3, "n3_l")
+        n4_l = load_list(n4, "n4_l")
+        w_raw = load_words(w1_words, "w_raw", nc.scalar, "b_picked")
+        x_two = pick_words(x_table, two_l, "x_two", "tokens")
+        d_k2 = pick_words(d_table, k2_l, "d_k2", "codes")
+        d_k2_dealt = tile([P, S], U32, "d_k2_dealt", "dealt")
+        deal_words(nc.vector.tensor_copy, d_k2_dealt, d_k2)
+        b_banks = product(d_k2_dealt, x_two, planes_b, "b_acc", 0)
+
+        w_dealt = tile([P, S], U32, "w_dealt")
+        deal_words(nc.scalar.copy, w_dealt, w_raw)
+        w_plane = tile([P, S], U8, "w_plane")
+        deal_bytes(nc.gpsimd.tensor_copy, w_plane[:], w_raw_bytes[:])
+
+        pick_scales(k1_l, offs_l, planes_a, nc.sync, "a_bytes", "codes")
+        d_k1 = pick_words(d_table, k1_l, "d_k1", "dealt")
+        x_offs = pick_words(x_table, offs_l, "x_offs", "tokens")
+        d_k1_dealt = tile([P, S], U32, "d_k1_dealt")
+        deal_words(nc.vector.tensor_copy, d_k1_dealt, d_k1)
+        a_banks = product(d_k1_dealt, x_offs, planes_a, "a_acc", PACK)
+
+
+        halves = [slice(HALF * h, HALF * (h + 1)) for h in range(2)]
+        list_halves = [slice(HALF // 16 * h, HALF // 16 * (h + 1)) for h in range(2)]
+
+        b_rows, b_far = [], []
+        for t in range(PACK):
+            rows = tile([P, S], F32, "b_rows%d" % t)
+            nc.scalar.activation(rows[:], b_banks[t][:], ACT.Copy, scale=0.0625)
+            far = tile([P, S], F32, "b_far%d" % t)
+            for h in range(2):
+                nc.scalar.activation(far[:, halves[h]], rows[:].indirect(n2_l[:, list_halves[h]]), ACT.Copy)
+            b_rows.append(rows)
+            b_far.append(far)
+
+        b_diff = []
+        for t in range(PACK):
+            diff = tile([P, S], F32, "b_diff%d" % t)
+            nc.vector.tensor_tensor(diff[:], b_far[t][:], b_rows[t][:], ALU.subtract)
+            b_diff.append(diff)
+
+        a_rows = []
+        for t in range(PACK):
+            rows = tile([P, S], F32, "a_rows%d" % t)
+            if t < A_ON_VECTOR:
+                nc.vector.tensor_scalar(rows[:], a_banks[t][:], gain_half[:, t : t + 1], None, ALU.mult)
+            else:
+                nc.scalar.activation(rows[:], a_banks[t][:], ACT.Copy, scale=gain_half[:, t : t + 1])
+            a_rows.append(rows)
+
+        z_codes, z_scales = [], []
+        for h in range(2):
+            z_planes = tile([P, PACK, HALF], BF16, "z_planes%d" % h)
+            for t in range(PACK):
+                col = slice(t, t + 1)
+                far = tile([P, HALF], F32, "a_far%d_%d" % (t, h))
+                gate = tile([P, HALF], F32, "gate%d_%d" % (t, h))
+                diff = tile([P, HALF], F32, "a_diff%d_%d" % (t, h))
+                pull = tile([P, HALF], F32, "pull%d_%d" % (t, h))
+                nc.scalar.activation(far[:], a_rows[t][:].indirect(n1_l[:, list_halves[h]]), ACT.Copy)
+                nc.scalar.activation(gate[:], b_diff[t][:, halves[h]], ACT.Tanh, scale=0.5)
+                nc.vector.scalar_tensor_tensor(diff[:], a_banks[t][:, halves[h]], gain_back[:, col], far[:], ALU.mult, ALU.add)
+                nc.vector.scalar_tensor_tensor(pull[:], gate[:], 1.0, diff[:], ALU.add, ALU.mult)
+                nc.vector.scalar_tensor_tensor(z_planes[:, t, :], a_banks[t][:, halves[h]], gain_full[:, col], pull[:], ALU.mult, ALU.add)
+            grouped = tile([P, HALF, PACK], BF16, "z_grouped%d" % h)
+            nc.vector.tensor_copy(
+                grouped[:].rearrange("p (c i) t -> p c t i", i=4),
+                z_planes[:].rearrange("p t (c i) -> p c t i", i=4),
+            )
+            codes = tile([P, HALF], U32, "z_codes%d" % h)
+            plane = tile([P, HALF], U8, "z_plane%d" % h)
+            nc.vector.quantize_mx(codes[:].bitcast(FP8X4), plane[:], grouped[:].rearrange("p w t -> p (w t)"))
+            z_codes.append(codes)
+            z_scales.append(plane)
+
+        h_rows = [tile([P, S], F32, "h_rows%d" % t) for t in range(PACK)]
+        for h in range(2):
+            for t in range(PACK):
+                acc = bank([P, HALF], "h_acc%d_%d" % (t, h), PACK * h + t)
+                cols = slice(P * t, P * (t + 1))
+                nc.tensor.matmul_mx(
+                    acc[:], lhsT=w_dealt[:, cols].bitcast(FP8X4), lhsT_scale=w_plane[:, cols],
+                    rhs=z_codes[h][:].bitcast(FP8X4), rhs_scale=z_scales[h][:], start=True, stop=True,
+                )
+                if h == 0:
+                    nc.scalar.activation(h_rows[t][:, halves[h]], acc[:], ACT.Copy)
+                else:
+                    nc.vector.tensor_copy(h_rows[t][:, halves[h]], acc[:])
+
+        y_grouped = tile([P, S, PACK], BF16, "y_grouped")
+        out_rows = out_0.rearrange("(p t) j -> p t j", t=PACK)
+        results = []
+
+        def fetch(t):
+            rows = h_rows[t]
+            sg2 = tile([P, HALF], F32, "sg2_%d" % t)
+            pa = tile([P, HALF], F32, "pa%d" % t)
+            sg = tile([P, HALF], F32, "sg_%d" % t)
+            pb = tile([P, HALF], F32, "pb%d" % t)
+            col = slice(t, t + 1)
+            nc.scalar.activation(sg2[:], rows[:].indirect(n4_l[:]), ACT.Sigmoid, bias=bias[:, col], scale=slope[:, col])
+            nc.scalar.activation(pa[:], rows[:].indirect(n3_l[:]), ACT.Copy)
+            nc.scalar.activation(sg[:], rows[:].indirect(n3_l[:]), ACT.Sigmoid, bias=bias[:, col], scale=slope[:, col])
+            nc.scalar.activation(pb[:], rows[:].indirect(n4_l[:]), ACT.Copy)
+            ra = tile([P, HALF], F32, "ra%d" % t)
+            rb = tile([P, HALF], F32, "rb%d" % t)
+            nc.vector.tensor_tensor(ra[:], pa[:], sg2[:], ALU.mult)
+            nc.vector.tensor_tensor(rb[:], pb[:], sg[:], ALU.subtract)
+            results.append((ra, rb))
+
+        def put(t):
+            ra, rb = results[t]
+            y = tile([P, S], F32, "y%d" % t)
+            nc.scalar.activation(y[:].indirect(n3_l[:]), ra[:], ACT.Copy)
+            nc.scalar.activation(y[:].indirect(n4_l[:]), rb[:], ACT.Copy)
+            nc.sync.dma_start(out_rows[:, t, :], y[:])
+            for h in range(2):
+                nc.vector.tensor_copy(y_grouped[:, halves[h], t], y[:, halves[h]])
+
+        fetch(0)
+        for t in range(1, PACK):
+            fetch(t)
+            put(t - 1)
+        put(PACK - 1)
+
+        y_codes = tile([P, S], U32, "y_codes")
+        y_plane = tile([P, S], U8, "y_plane")
+        words_out = out_1[0].rearrange("p n t -> p (n t)").bitcast(I32)
+        for h in range(2):
+            nc.vector.quantize_mx(
+                y_codes[:, halves[h]].bitcast(FP8X4), y_plane[:, halves[h]],
+                y_grouped[:, halves[h], :].rearrange("p w t -> p (w t)"),
+            )
+            nc.sync.dma_start(words_out[:, halves[h]], y_codes[:, halves[h]].bitcast(I32))
+        for q in range(4):
+            queue = nc.scalar if q % 2 else nc.sync
+            queue.dma_start(out_2[0, 4 * q : 4 * q + 4, :].bitcast(I32), y_plane[32 * q : 32 * q + 4, :].bitcast(I32))

@@ -72,6 +72,8 @@ def tile_picked_twpqpullbeod_none_po_kernel(
         d_table = load_words(d_words, "d_table", nc.sync)
 
         gain = load_column(gn, "gain")
+        warm = tile([P, 1], F32, "warm")
+        nc.scalar.activation(warm[:], gain[:, 0:1], ACT.Sigmoid)
         slope = load_column(sl, "slope")
         thresh = load_column(th, "thresh")
         gain_full = tile([P, PACK], F32, "gain_full")

@@ -19,7 +19,24 @@ HALF = S // 2
 T, G = 1024, 2048
 ROWS = 16
 ALIGN = 64
-A_ON_VECTOR = 2
+A_ON_VECTOR = 4
+U_G = 0
+ORD = 0
+EARLY = 2
+PRE = 4
+U0 = 0
+IL_S = 0
+WIDTHS = [256, 256]
+LATE = 4
+DB_G = ()
+HOLD = 0
+RING = 8
+MOVE_A2 = 0
+D_FIRST = 0
+W_TAG = "w_dealt"
+BCAST = 0
+MS_G = 1
+GRING = 8
 
 FLOPS = 3 * 2 * 512 * 512 * 512
 
@@ -53,8 +70,11 @@ def tile_picked_twpqpullbeod_none_po_kernel(
         def load_scale_window(src, name):
             width = src.shape[2]
             held = tile([P, width], U8, name)
-            rows = src[0].bitcast(I32).unsqueeze(1).to_broadcast([ROWS, P // ROWS, width // 4])
-            nc.sync.dma_start(held[:].bitcast(I32), rows)
+            if BCAST:
+                nc.sync.dma_start(held[:].bitcast(I32), src[0].bitcast(I32).unsqueeze(1).to_broadcast([ROWS, P // ROWS, width // 4]))
+                return held
+            (nc.gpsimd if width == G else nc.vector).memset(held[:].bitcast(I32), 0)
+            nc.sync.dma_start(held[0 : P : P // ROWS, :].bitcast(I32), src[0].bitcast(I32))
             return held
 
         def load_column(src, name):
@@ -62,14 +82,22 @@ def tile_picked_twpqpullbeod_none_po_kernel(
             nc.gpsimd.dma_start(held[:], src.rearrange("(p t) o -> p (t o)", t=PACK))
             return held
 
-        k2_l = load_list(k2, "k2_l")
-        d_bytes = load_scale_window(d_scales, "d_bytes")
         two_l = load_list(two, "two_l")
+        k2_l = load_list(k2, "k2_l")
+        if ORD == 1:
+            k1_l = load_list(k1, "k1_l")
+            offs_l = load_list(offs, "offs_l")
         x_bytes = load_scale_window(x_scales, "x_bytes")
-        k1_l = load_list(k1, "k1_l")
-        offs_l = load_list(offs, "offs_l")
+        d_bytes = load_scale_window(d_scales, "d_bytes")
+        if ORD == 2:
+            k1_l = load_list(k1, "k1_l")
+            offs_l = load_list(offs, "offs_l")
         x_table = load_words(x_words, "x_table", nc.sync)
         d_table = load_words(d_words, "d_table", nc.sync)
+        if ORD == 0:
+            k1_l = load_list(k1, "k1_l")
+            offs_l = load_list(offs, "offs_l")
+        w_raw = load_words(w1_words, "w_raw", nc.sync)
 
         gain = load_column(gn, "gain")
         warm = tile([P, 1], F32, "warm")
@@ -77,9 +105,8 @@ def tile_picked_twpqpullbeod_none_po_kernel(
         slope = load_column(sl, "slope")
         thresh = load_column(th, "thresh")
         gain_full = tile([P, PACK], F32, "gain_full")
-        gain_half = tile([P, PACK], F32, "gain_half")
         gain_back = tile([P, PACK], F32, "gain_back")
-        for scaled, factor in ((gain_half, 0.03125), (gain_back, -0.03125), (gain_full, 0.0625)):
+        for scaled, factor in ((gain_full, 0.0625), (gain_back, -0.0625)):
             nc.gpsimd.tensor_scalar(scaled[:], gain[:], factor, 0.0, ALU.mult, ALU.add)
         shift = tile([P, PACK], F32, "shift")
         nc.gpsimd.tensor_tensor(shift[:], slope[:], thresh[:], ALU.mult)
@@ -109,7 +136,7 @@ def tile_picked_twpqpullbeod_none_po_kernel(
             deal_bytes(nc.vector.tensor_copy, dealt[:, :S], picked[:, :S])
             nc.vector.tensor_copy(dealt[:, S:].bitcast(I32), picked[:, S:].bitcast(I32))
             for v in range(4):
-                queue.dma_start(planes[v:P:32, :].bitcast(I32), dealt[8 * v : P : 32, :].bitcast(I32))
+                (nc.scalar if MOVE_A2 and v % 2 else queue).dma_start(planes[v:P:32, :].bitcast(I32), dealt[8 * v : P : 32, :].bitcast(I32))
 
         def pick_words(table, which, name, tag):
             picked = tile([P, S], U32, name, tag)
@@ -130,22 +157,23 @@ def tile_picked_twpqpullbeod_none_po_kernel(
 
         pick_scales(k2_l, two_l, planes_b, nc.sync, "b_bytes", "b_picked")
         n2_l = load_list(n2, "n2_l")
-        n1_l = load_list(n1, "n1_l")
-        n3_l = load_list(n3, "n3_l")
-        n4_l = load_list(n4, "n4_l")
-        w_raw = load_words(w1_words, "w_raw", nc.scalar, "b_picked")
-        x_two = pick_words(x_table, two_l, "x_two", "tokens")
-        d_k2 = pick_words(d_table, k2_l, "d_k2", "codes")
+        if D_FIRST:
+            d_k2 = pick_words(d_table, k2_l, "d_k2", "codes")
+            x_two = pick_words(x_table, two_l, "x_two", "tokens")
+        else:
+            x_two = pick_words(x_table, two_l, "x_two", "tokens")
+            d_k2 = pick_words(d_table, k2_l, "d_k2", "codes")
         d_k2_dealt = tile([P, S], U32, "d_k2_dealt", "dealt")
         deal_words(nc.vector.tensor_copy, d_k2_dealt, d_k2)
         b_banks = product(d_k2_dealt, x_two, planes_b, "b_acc", 0)
 
-        w_dealt = tile([P, S], U32, "w_dealt")
-        deal_words(nc.scalar.copy, w_dealt, w_raw)
         w_plane = tile([P, S], U8, "w_plane")
         deal_bytes(nc.gpsimd.tensor_copy, w_plane[:], w_raw_bytes[:])
 
         pick_scales(k1_l, offs_l, planes_a, nc.sync, "a_bytes", "codes")
+        n1_l = load_list(n1, "n1_l")
+        n3_l = load_list(n3, "n3_l")
+        n4_l = load_list(n4, "n4_l")
         d_k1 = pick_words(d_table, k1_l, "d_k1", "dealt")
         x_offs = pick_words(x_table, offs_l, "x_offs", "tokens")
         d_k1_dealt = tile([P, S], U32, "d_k1_dealt")
@@ -167,58 +195,80 @@ def tile_picked_twpqpullbeod_none_po_kernel(
             b_far.append(far)
 
         b_diff = []
-        for t in range(PACK):
-            diff = tile([P, S], F32, "b_diff%d" % t)
-            nc.vector.tensor_tensor(diff[:], b_far[t][:], b_rows[t][:], ALU.subtract)
+
+        def gate_input(t):
+            diff = tile([P, S], F32, "b_diff%d" % t, {2: "tokens", 3: "d_k1_dealt"}.get(t) if t >= LATE else None)
+            if t in DB_G:
+                nc.gpsimd.tensor_tensor(diff[:], b_far[t][:], b_rows[t][:], ALU.subtract)
+            else:
+                nc.vector.scalar_tensor_tensor(diff[:], b_banks[t][:], -0.0625, b_far[t][:], ALU.mult, ALU.add)
             b_diff.append(diff)
 
+        for t in range(EARLY):
+            gate_input(t)
+
         a_rows = []
-        for t in range(PACK):
-            rows = tile([P, S], F32, "a_rows%d" % t)
+
+        def empty_a(t):
             if t < A_ON_VECTOR:
-                nc.vector.tensor_scalar(rows[:], a_banks[t][:], gain_half[:, t : t + 1], None, ALU.mult)
+                rows = tile([P, S], F32, "a_rows%d" % t)
+                nc.vector.tensor_scalar(rows[:], a_banks[t][:], gain_full[:, t : t + 1], None, ALU.mult)
             else:
-                nc.scalar.activation(rows[:], a_banks[t][:], ACT.Copy, scale=gain_half[:, t : t + 1])
+                rows = tile([P, S], F32, "a_rows%d" % t, "a_first%d" % (t - A_ON_VECTOR) if HOLD else None)
+                nc.scalar.activation(rows[:], a_banks[t][:], ACT.Copy, scale=gain_full[:, t : t + 1])
             a_rows.append(rows)
 
+        for t in range(PRE):
+            empty_a(t)
+        for t in range(EARLY, PACK):
+            gate_input(t)
         z_codes, z_scales = [], []
-        for h in range(2):
-            z_planes = tile([P, PACK, HALF], BF16, "z_planes%d" % h)
+        diff_ring = tile([P, RING, HALF], F32, "diff_ring")
+        gate_ring = tile([P, GRING, HALF], F32, "gate_ring")
+        starts = [sum(WIDTHS[:h]) for h in range(len(WIDTHS))]
+        spans = [slice(s, s + w) for s, w in zip(starts, WIDTHS)]
+        for h, (span, width) in enumerate(zip(spans, WIDTHS)):
+            entries = slice(span.start // 16, span.stop // 16)
+            far = tile([P, PACK, width], F32, "a_far%d" % h)
+            pull = tile([P, PACK, width], F32, "pull%d" % h)
             for t in range(PACK):
                 col = slice(t, t + 1)
-                far = tile([P, HALF], F32, "a_far%d_%d" % (t, h))
-                gate = tile([P, HALF], F32, "gate%d_%d" % (t, h))
-                diff = tile([P, HALF], F32, "a_diff%d_%d" % (t, h))
-                pull = tile([P, HALF], F32, "pull%d_%d" % (t, h))
-                nc.scalar.activation(far[:], a_rows[t][:].indirect(n1_l[:, list_halves[h]]), ACT.Copy)
-                nc.scalar.activation(gate[:], b_diff[t][:, halves[h]], ACT.Tanh, scale=0.5)
-                nc.vector.scalar_tensor_tensor(diff[:], a_banks[t][:, halves[h]], gain_back[:, col], far[:], ALU.mult, ALU.add)
-                nc.vector.scalar_tensor_tensor(pull[:], gate[:], 1.0, diff[:], ALU.add, ALU.mult)
-                nc.vector.scalar_tensor_tensor(z_planes[:, t, :], a_banks[t][:, halves[h]], gain_full[:, col], pull[:], ALU.mult, ALU.add)
-            grouped = tile([P, HALF, PACK], BF16, "z_grouped%d" % h)
-            nc.vector.tensor_copy(
+                if h == 0 and t >= PRE:
+                    empty_a(t)
+                gate = gate_ring[:, (4 * h + t) % GRING, :width]
+                diff = diff_ring[:, (4 * h + t) % RING, :width]
+                nc.scalar.activation(far[:, t, :], a_rows[t][:].indirect(n1_l[:, entries]), ACT.Copy)
+                nc.scalar.activation(gate, b_diff[t][:, span], ACT.Sigmoid, scale=-1.0)
+                nc.vector.scalar_tensor_tensor(diff, a_banks[t][:, span], gain_back[:, col], far[:, t, :], ALU.mult, ALU.add)
+                (nc.gpsimd if U0 <= 4 * h + t < U_G else nc.vector).tensor_tensor(pull[:, t, :], gate, diff, ALU.mult)
+            grouped = tile([P, width, PACK], BF16, "z_grouped%d" % h)
+            nc.vector.tensor_tensor(
                 grouped[:].rearrange("p (c i) t -> p c t i", i=4),
-                z_planes[:].rearrange("p t (c i) -> p c t i", i=4),
+                far[:].rearrange("p t (c i) -> p c t i", i=4),
+                pull[:].rearrange("p t (c i) -> p c t i", i=4),
+                ALU.subtract,
             )
-            codes = tile([P, HALF], U32, "z_codes%d" % h)
-            plane = tile([P, HALF], U8, "z_plane%d" % h)
+            codes = tile([P, width], U32, "z_codes%d" % h)
+            plane = tile([P, width], U8, "z_plane%d" % h)
             nc.vector.quantize_mx(codes[:].bitcast(FP8X4), plane[:], grouped[:].rearrange("p w t -> p (w t)"))
             z_codes.append(codes)
             z_scales.append(plane)
 
+        w_dealt = tile([P, S], U32, "w_dealt")
+        deal_words(nc.scalar.copy, w_dealt, w_raw)
         h_rows = [tile([P, S], F32, "h_rows%d" % t) for t in range(PACK)]
-        for h in range(2):
+        h_banks = [bank([P, S], "h_acc%d" % t, t) for t in range(PACK)]
+        for h, span in enumerate(spans):
             for t in range(PACK):
-                acc = bank([P, HALF], "h_acc%d_%d" % (t, h), PACK * h + t)
                 cols = slice(P * t, P * (t + 1))
                 nc.tensor.matmul_mx(
-                    acc[:], lhsT=w_dealt[:, cols].bitcast(FP8X4), lhsT_scale=w_plane[:, cols],
+                    h_banks[t][:, span], lhsT=w_dealt[:, cols].bitcast(FP8X4), lhsT_scale=w_plane[:, cols],
                     rhs=z_codes[h][:].bitcast(FP8X4), rhs_scale=z_scales[h][:], start=True, stop=True,
                 )
-                if h == 0:
-                    nc.scalar.activation(h_rows[t][:, halves[h]], acc[:], ACT.Copy)
+                if h < len(spans) - 1 or t == 0:
+                    nc.scalar.activation(h_rows[t][:, span], h_banks[t][:, span], ACT.Copy)
                 else:
-                    nc.vector.tensor_copy(h_rows[t][:, halves[h]], acc[:])
+                    nc.vector.tensor_copy(h_rows[t][:, span], h_banks[t][:, span])
 
         y_grouped = tile([P, S, PACK], BF16, "y_grouped")
         out_rows = out_0.rearrange("(p t) j -> p t j", t=PACK)

@@ -14,29 +14,16 @@ ACT = mybir.ActivationFunctionType
 
 P = 128
 PACK = 4
+QUADS = 4
+SCALE_ROWS = 16
 S = 512
 HALF = S // 2
-T, G = 1024, 2048
-ROWS = 16
+PER_COLUMN = 16
+LINE = 4
 ALIGN = 64
-A_ON_VECTOR = 4
-U_G = 0
-ORD = 0
-EARLY = 2
-PRE = 4
-U0 = 0
-IL_S = 0
-WIDTHS = [256, 256]
-LATE = 4
-DB_G = ()
-HOLD = 0
-RING = 8
-MOVE_A2 = 0
-D_FIRST = 0
-W_TAG = "w_dealt"
-BCAST = 0
-MS_G = 1
-GRING = 8
+SIXTEENTH = 0.0625
+
+Z_SPANS = (slice(0, 128), slice(128, 384), slice(384, 512))
 
 FLOPS = 3 * 2 * 512 * 512 * 512
 
@@ -48,224 +35,195 @@ def tile_picked_twpqpullbeod_none_po_kernel(
     nc = tc.nc
     with ExitStack() as ctx:
         lists = ctx.enter_context(tc.tile_pool(name="lists", bufs=1))
-        sb = ctx.enter_context(tc.tile_pool(name="sb", bufs=1))
+        sbuf = ctx.enter_context(tc.tile_pool(name="sbuf", bufs=1))
         psum = ctx.enter_context(tc.psum_pool(name="psum", bufs=1))
 
         def tile(shape, dtype, name, tag=None):
-            return sb.tile(shape, dtype, name=name, tag=tag or name, align_bytes=ALIGN)
+            return sbuf.tile(shape, dtype, name=name, tag=tag or name, align_bytes=ALIGN)
 
-        def bank(shape, name, index):
-            return psum.tile(shape, F32, name=name, tag="bank%d" % index)
+        def bank(name, index):
+            return psum.tile([P, S], F32, name=name, tag="bank%d" % index)
+
+        def entries(span):
+            return slice(span.start // PER_COLUMN, span.stop // PER_COLUMN)
 
         def load_list(src, name):
             held = lists.tile(list(src.shape), U16, name=name)
             nc.sync.dma_start(held[:], src)
             return held
 
-        def load_words(src, name, queue, tag=None):
-            held = tile([P, src.shape[2]], U32, name, tag)
-            queue.dma_start(held[:].bitcast(I32), src[0].rearrange("p n t -> p (n t)").bitcast(I32))
+        def load_words(src, name):
+            held = tile([P, src.shape[2]], U32, name)
+            nc.sync.dma_start(held[:].bitcast(I32), src[0].rearrange("p n t -> p (n t)").bitcast(I32))
             return held
 
-        def load_scale_window(src, name):
-            width = src.shape[2]
+        def zeroed_bytes(width, name, engine):
             held = tile([P, width], U8, name)
-            if BCAST:
-                nc.sync.dma_start(held[:].bitcast(I32), src[0].bitcast(I32).unsqueeze(1).to_broadcast([ROWS, P // ROWS, width // 4]))
-                return held
-            (nc.gpsimd if width == G else nc.vector).memset(held[:].bitcast(I32), 0)
-            nc.sync.dma_start(held[0 : P : P // ROWS, :].bitcast(I32), src[0].bitcast(I32))
+            engine.memset(held[:].bitcast(I32), 0)
             return held
 
-        def load_column(src, name):
+        def load_plane(held, src, queue):
+            for q in range(QUADS):
+                queue.dma_start(held[32 * q : 32 * q + 4, :].bitcast(I32), src[0, 4 * q : 4 * q + 4, :].bitcast(I32))
+
+        def load_spread(held, src):
+            nc.sync.dma_start(held[0 : P : P // SCALE_ROWS, :].bitcast(I32), src[0].bitcast(I32))
+
+        def load_row_values(src, name):
             held = tile([P, PACK], F32, name)
             nc.gpsimd.dma_start(held[:], src.rearrange("(p t) o -> p (t o)", t=PACK))
             return held
 
+        def deal_words(copy, dst, src):
+            copy(
+                dst[:].rearrange("p (t c i) -> p c t i", t=PACK, i=LINE),
+                src[:].rearrange("p (c i t) -> p c t i", t=PACK, i=LINE),
+            )
+
+        def deal_bytes(copy, dst, src):
+            copy(dst.rearrange("p (t m) -> p t m", t=PACK), src.rearrange("p (m t) -> p t m", t=PACK))
+
         two_l = load_list(two, "two_l")
         k2_l = load_list(k2, "k2_l")
-        if ORD == 1:
-            k1_l = load_list(k1, "k1_l")
-            offs_l = load_list(offs, "offs_l")
-        x_bytes = load_scale_window(x_scales, "x_bytes")
-        d_bytes = load_scale_window(d_scales, "d_bytes")
-        if ORD == 2:
-            k1_l = load_list(k1, "k1_l")
-            offs_l = load_list(offs, "offs_l")
-        x_table = load_words(x_words, "x_table", nc.sync)
-        d_table = load_words(d_words, "d_table", nc.sync)
-        if ORD == 0:
-            k1_l = load_list(k1, "k1_l")
-            offs_l = load_list(offs, "offs_l")
-        w_raw = load_words(w1_words, "w_raw", nc.sync)
+        d_bytes = zeroed_bytes(d_scales.shape[2], "d_bytes", nc.gpsimd)
+        load_spread(d_bytes, d_scales)
+        x_bytes = zeroed_bytes(x_scales.shape[2], "x_bytes", nc.vector)
+        load_plane(x_bytes, x_scales, nc.sync)
+        x_table = load_words(x_words, "x_table")
+        d_table = load_words(d_words, "d_table")
+        k1_l = load_list(k1, "k1_l")
+        offs_l = load_list(offs, "offs_l")
+        w_raw = load_words(w1_words, "w_raw")
 
-        gain = load_column(gn, "gain")
+        gain = load_row_values(gn, "gain")
         warm = tile([P, 1], F32, "warm")
         nc.scalar.activation(warm[:], gain[:, 0:1], ACT.Sigmoid)
-        slope = load_column(sl, "slope")
-        thresh = load_column(th, "thresh")
-        gain_full = tile([P, PACK], F32, "gain_full")
-        gain_back = tile([P, PACK], F32, "gain_back")
-        for scaled, factor in ((gain_full, 0.0625), (gain_back, -0.0625)):
+        slope = load_row_values(sl, "slope")
+        thresh = load_row_values(th, "thresh")
+        gain_up = tile([P, PACK], F32, "gain_up")
+        gain_down = tile([P, PACK], F32, "gain_down")
+        for scaled, factor in ((gain_up, SIXTEENTH), (gain_down, -SIXTEENTH)):
             nc.gpsimd.tensor_scalar(scaled[:], gain[:], factor, 0.0, ALU.mult, ALU.add)
         shift = tile([P, PACK], F32, "shift")
         nc.gpsimd.tensor_tensor(shift[:], slope[:], thresh[:], ALU.mult)
         bias = tile([P, PACK], F32, "bias")
         nc.gpsimd.tensor_scalar(bias[:], shift[:], -1.0, 0.0, ALU.mult, ALU.add)
-        w_raw_bytes = tile([P, S], U8, "w_raw_bytes")
-        nc.gpsimd.memset(w_raw_bytes[:].bitcast(I32), 0)
-        for q in range(4):
-            nc.gpsimd.dma_start(w_raw_bytes[32 * q : 32 * q + 4, :].bitcast(I32), w1_scales[0, 4 * q : 4 * q + 4, :].bitcast(I32))
+        w_raw_bytes = zeroed_bytes(S, "w_raw_bytes", nc.gpsimd)
+        load_plane(w_raw_bytes, w1_scales, nc.gpsimd)
 
-        planes_b = tile([P, 2 * S], U8, "planes_b")
-        planes_a = tile([P, 2 * S], U8, "planes_a")
-        nc.vector.memset(planes_b[:].bitcast(I32), 0)
-        nc.vector.memset(planes_a[:].bitcast(I32), 0)
+        b_plane = zeroed_bytes(S, "b_plane", nc.vector)
+        a_plane = zeroed_bytes(S, "a_plane", nc.vector)
 
-        def deal_words(engine_copy, dst, src):
-            engine_copy(dst[:].rearrange("p (t c i) -> p c t i", t=PACK, i=4), src[:].rearrange("p (c i t) -> p c t i", t=PACK, i=4))
-
-        def deal_bytes(engine_copy, dst, src):
-            engine_copy(dst.rearrange("p (t m) -> p t m", t=PACK), src.rearrange("p (m t) -> p t m", t=PACK))
-
-        def pick_scales(d_list, x_list, planes, queue, name, tag):
+        def pick_scales(d_list, x_list, plane, name, tag):
             picked = tile([P, 2 * S], U8, name + "_picked", tag)
             nc.vector.tensor_copy(picked[:, :S], d_bytes[:].indirect(d_list[:]))
             nc.vector.tensor_copy(picked[:, S:], x_bytes[:].indirect(x_list[:]))
-            dealt = tile([P, 2 * S], U8, name + "_dealt")
-            deal_bytes(nc.vector.tensor_copy, dealt[:, :S], picked[:, :S])
-            nc.vector.tensor_copy(dealt[:, S:].bitcast(I32), picked[:, S:].bitcast(I32))
+            dealt = tile([P, S], U8, name + "_dealt")
+            deal_bytes(nc.vector.tensor_copy, dealt[:], picked[:, :S])
             for v in range(4):
-                (nc.scalar if MOVE_A2 and v % 2 else queue).dma_start(planes[v:P:32, :].bitcast(I32), dealt[8 * v : P : 32, :].bitcast(I32))
+                nc.sync.dma_start(plane[v:P:32, :].bitcast(I32), dealt[8 * v : P : 32, :].bitcast(I32))
+            return picked[:, S:]
 
         def pick_words(table, which, name, tag):
             picked = tile([P, S], U32, name, tag)
             nc.vector.tensor_copy(picked[:], table[:].indirect(which[:]))
             return picked
 
-        def product(dealt, moving, planes, name, first_bank):
+        def product(d_dealt, d_plane, x_picked, x_plane, name, first_bank):
             banks = []
             for t in range(PACK):
-                acc = bank([P, S], "%s%d" % (name, t), first_bank + t)
+                acc = bank("%s%d" % (name, t), first_bank + t)
                 cols = slice(P * t, P * (t + 1))
                 nc.tensor.matmul_mx(
-                    acc[:], lhsT=dealt[:, cols].bitcast(FP8X4), lhsT_scale=planes[:, cols],
-                    rhs=moving[:].bitcast(FP8X4), rhs_scale=planes[:, S:], start=True, stop=True,
+                    acc[:], lhsT=d_dealt[:, cols].bitcast(FP8X4), lhsT_scale=d_plane[:, cols],
+                    rhs=x_picked[:].bitcast(FP8X4), rhs_scale=x_plane, start=True, stop=True,
                 )
                 banks.append(acc)
             return banks
 
-        pick_scales(k2_l, two_l, planes_b, nc.sync, "b_bytes", "b_picked")
+        b_x_plane = pick_scales(k2_l, two_l, b_plane, "b_bytes", None)
         n2_l = load_list(n2, "n2_l")
-        if D_FIRST:
-            d_k2 = pick_words(d_table, k2_l, "d_k2", "codes")
-            x_two = pick_words(x_table, two_l, "x_two", "tokens")
-        else:
-            x_two = pick_words(x_table, two_l, "x_two", "tokens")
-            d_k2 = pick_words(d_table, k2_l, "d_k2", "codes")
-        d_k2_dealt = tile([P, S], U32, "d_k2_dealt", "dealt")
+        x_two = pick_words(x_table, two_l, "x_two", "x_picked")
+        d_k2 = pick_words(d_table, k2_l, "d_k2", "d_picked")
+        d_k2_dealt = tile([P, S], U32, "d_k2_dealt", "d_dealt")
         deal_words(nc.vector.tensor_copy, d_k2_dealt, d_k2)
-        b_banks = product(d_k2_dealt, x_two, planes_b, "b_acc", 0)
+        b_banks = product(d_k2_dealt, b_plane, x_two, b_x_plane, "b_acc", 0)
 
         w_plane = tile([P, S], U8, "w_plane")
         deal_bytes(nc.gpsimd.tensor_copy, w_plane[:], w_raw_bytes[:])
 
-        pick_scales(k1_l, offs_l, planes_a, nc.sync, "a_bytes", "codes")
+        a_x_plane = pick_scales(k1_l, offs_l, a_plane, "a_bytes", "d_picked")
         n1_l = load_list(n1, "n1_l")
         n3_l = load_list(n3, "n3_l")
         n4_l = load_list(n4, "n4_l")
-        d_k1 = pick_words(d_table, k1_l, "d_k1", "dealt")
-        x_offs = pick_words(x_table, offs_l, "x_offs", "tokens")
+        d_k1 = pick_words(d_table, k1_l, "d_k1", "d_dealt")
+        x_offs = pick_words(x_table, offs_l, "x_offs", "x_picked")
         d_k1_dealt = tile([P, S], U32, "d_k1_dealt")
         deal_words(nc.vector.tensor_copy, d_k1_dealt, d_k1)
-        a_banks = product(d_k1_dealt, x_offs, planes_a, "a_acc", PACK)
-
+        a_banks = product(d_k1_dealt, a_plane, x_offs, a_x_plane, "a_acc", PACK)
 
         halves = [slice(HALF * h, HALF * (h + 1)) for h in range(2)]
-        list_halves = [slice(HALF // 16 * h, HALF // 16 * (h + 1)) for h in range(2)]
-
-        b_rows, b_far = [], []
+        b_far = []
         for t in range(PACK):
-            rows = tile([P, S], F32, "b_rows%d" % t)
-            nc.scalar.activation(rows[:], b_banks[t][:], ACT.Copy, scale=0.0625)
+            b_rows = tile([P, S], F32, "b_rows%d" % t)
+            nc.scalar.activation(b_rows[:], b_banks[t][:], ACT.Copy, scale=SIXTEENTH)
             far = tile([P, S], F32, "b_far%d" % t)
-            for h in range(2):
-                nc.scalar.activation(far[:, halves[h]], rows[:].indirect(n2_l[:, list_halves[h]]), ACT.Copy)
-            b_rows.append(rows)
+            for half in halves:
+                nc.scalar.activation(far[:, half], b_rows[:].indirect(n2_l[:, entries(half)]), ACT.Copy)
             b_far.append(far)
 
-        b_diff = []
+        b_diff = [tile([P, S], F32, "b_diff%d" % t) for t in range(PACK)]
+        a_rows = [tile([P, S], F32, "a_rows%d" % t) for t in range(PACK)]
 
-        def gate_input(t):
-            diff = tile([P, S], F32, "b_diff%d" % t, {2: "tokens", 3: "d_k1_dealt"}.get(t) if t >= LATE else None)
-            if t in DB_G:
-                nc.gpsimd.tensor_tensor(diff[:], b_far[t][:], b_rows[t][:], ALU.subtract)
-            else:
-                nc.vector.scalar_tensor_tensor(diff[:], b_banks[t][:], -0.0625, b_far[t][:], ALU.mult, ALU.add)
-            b_diff.append(diff)
+        def subtract_b(t):
+            nc.vector.scalar_tensor_tensor(b_diff[t][:], b_banks[t][:], -SIXTEENTH, b_far[t][:], ALU.mult, ALU.add)
 
-        for t in range(EARLY):
-            gate_input(t)
+        for t in range(PACK // 2):
+            subtract_b(t)
+        for t in range(PACK):
+            nc.vector.tensor_scalar(a_rows[t][:], a_banks[t][:], gain_up[:, t : t + 1], None, ALU.mult)
+        for t in range(PACK // 2, PACK):
+            subtract_b(t)
 
-        a_rows = []
-
-        def empty_a(t):
-            if t < A_ON_VECTOR:
-                rows = tile([P, S], F32, "a_rows%d" % t)
-                nc.vector.tensor_scalar(rows[:], a_banks[t][:], gain_full[:, t : t + 1], None, ALU.mult)
-            else:
-                rows = tile([P, S], F32, "a_rows%d" % t, "a_first%d" % (t - A_ON_VECTOR) if HOLD else None)
-                nc.scalar.activation(rows[:], a_banks[t][:], ACT.Copy, scale=gain_full[:, t : t + 1])
-            a_rows.append(rows)
-
-        for t in range(PRE):
-            empty_a(t)
-        for t in range(EARLY, PACK):
-            gate_input(t)
-        z_codes, z_scales = [], []
-        diff_ring = tile([P, RING, HALF], F32, "diff_ring")
-        gate_ring = tile([P, GRING, HALF], F32, "gate_ring")
-        starts = [sum(WIDTHS[:h]) for h in range(len(WIDTHS))]
-        spans = [slice(s, s + w) for s, w in zip(starts, WIDTHS)]
-        for h, (span, width) in enumerate(zip(spans, WIDTHS)):
-            entries = slice(span.start // 16, span.stop // 16)
-            far = tile([P, PACK, width], F32, "a_far%d" % h)
-            pull = tile([P, PACK, width], F32, "pull%d" % h)
+        z_codes, z_planes = [], []
+        for index, span in enumerate(Z_SPANS):
+            width = span.stop - span.start
+            a_far = tile([P, PACK, width], F32, "a_far%d" % index)
+            stay = tile([P, PACK, width], F32, "stay%d" % index)
+            a_diff = tile([P, PACK, width], F32, "a_diff%d" % index)
+            back = tile([P, PACK, width], F32, "back%d" % index)
             for t in range(PACK):
-                col = slice(t, t + 1)
-                if h == 0 and t >= PRE:
-                    empty_a(t)
-                gate = gate_ring[:, (4 * h + t) % GRING, :width]
-                diff = diff_ring[:, (4 * h + t) % RING, :width]
-                nc.scalar.activation(far[:, t, :], a_rows[t][:].indirect(n1_l[:, entries]), ACT.Copy)
-                nc.scalar.activation(gate, b_diff[t][:, span], ACT.Sigmoid, scale=-1.0)
-                nc.vector.scalar_tensor_tensor(diff, a_banks[t][:, span], gain_back[:, col], far[:, t, :], ALU.mult, ALU.add)
-                (nc.gpsimd if U0 <= 4 * h + t < U_G else nc.vector).tensor_tensor(pull[:, t, :], gate, diff, ALU.mult)
-            grouped = tile([P, width, PACK], BF16, "z_grouped%d" % h)
+                nc.scalar.activation(a_far[:, t, :], a_rows[t][:].indirect(n1_l[:, entries(span)]), ACT.Copy)
+                nc.scalar.activation(stay[:, t, :], b_diff[t][:, span], ACT.Sigmoid, scale=-1.0)
+                nc.vector.scalar_tensor_tensor(
+                    a_diff[:, t, :], a_banks[t][:, span], gain_down[:, t : t + 1], a_far[:, t, :], ALU.mult, ALU.add
+                )
+                nc.vector.tensor_tensor(back[:, t, :], stay[:, t, :], a_diff[:, t, :], ALU.mult)
+            z_grouped = tile([P, width, PACK], BF16, "z_grouped%d" % index)
             nc.vector.tensor_tensor(
-                grouped[:].rearrange("p (c i) t -> p c t i", i=4),
-                far[:].rearrange("p t (c i) -> p c t i", i=4),
-                pull[:].rearrange("p t (c i) -> p c t i", i=4),
+                z_grouped[:].rearrange("p (c i) t -> p c t i", i=LINE),
+                a_far[:].rearrange("p t (c i) -> p c t i", i=LINE),
+                back[:].rearrange("p t (c i) -> p c t i", i=LINE),
                 ALU.subtract,
             )
-            codes = tile([P, width], U32, "z_codes%d" % h)
-            plane = tile([P, width], U8, "z_plane%d" % h)
-            nc.vector.quantize_mx(codes[:].bitcast(FP8X4), plane[:], grouped[:].rearrange("p w t -> p (w t)"))
+            codes = tile([P, width], U32, "z_codes%d" % index)
+            plane = tile([P, width], U8, "z_plane%d" % index)
+            nc.vector.quantize_mx(codes[:].bitcast(FP8X4), plane[:], z_grouped[:].rearrange("p w t -> p (w t)"))
             z_codes.append(codes)
-            z_scales.append(plane)
+            z_planes.append(plane)
 
         w_dealt = tile([P, S], U32, "w_dealt")
         deal_words(nc.scalar.copy, w_dealt, w_raw)
         h_rows = [tile([P, S], F32, "h_rows%d" % t) for t in range(PACK)]
-        h_banks = [bank([P, S], "h_acc%d" % t, t) for t in range(PACK)]
-        for h, span in enumerate(spans):
+        h_banks = [bank("h_acc%d" % t, t) for t in range(PACK)]
+        for index, span in enumerate(Z_SPANS):
             for t in range(PACK):
                 cols = slice(P * t, P * (t + 1))
                 nc.tensor.matmul_mx(
                     h_banks[t][:, span], lhsT=w_dealt[:, cols].bitcast(FP8X4), lhsT_scale=w_plane[:, cols],
-                    rhs=z_codes[h][:].bitcast(FP8X4), rhs_scale=z_scales[h][:], start=True, stop=True,
+                    rhs=z_codes[index][:].bitcast(FP8X4), rhs_scale=z_planes[index][:], start=True, stop=True,
                 )
-                if h < len(spans) - 1 or t == 0:
+                if index < len(Z_SPANS) - 1 or t == 0:
                     nc.scalar.activation(h_rows[t][:, span], h_banks[t][:, span], ACT.Copy)
                 else:
                     nc.vector.tensor_copy(h_rows[t][:, span], h_banks[t][:, span])
@@ -275,12 +233,11 @@ def tile_picked_twpqpullbeod_none_po_kernel(
         results = []
 
         def fetch(t):
-            rows = h_rows[t]
+            rows, col = h_rows[t], slice(t, t + 1)
             sg2 = tile([P, HALF], F32, "sg2_%d" % t)
             pa = tile([P, HALF], F32, "pa%d" % t)
             sg = tile([P, HALF], F32, "sg_%d" % t)
             pb = tile([P, HALF], F32, "pb%d" % t)
-            col = slice(t, t + 1)
             nc.scalar.activation(sg2[:], rows[:].indirect(n4_l[:]), ACT.Sigmoid, bias=bias[:, col], scale=slope[:, col])
             nc.scalar.activation(pa[:], rows[:].indirect(n3_l[:]), ACT.Copy)
             nc.scalar.activation(sg[:], rows[:].indirect(n3_l[:]), ACT.Sigmoid, bias=bias[:, col], scale=slope[:, col])
@@ -297,8 +254,8 @@ def tile_picked_twpqpullbeod_none_po_kernel(
             nc.scalar.activation(y[:].indirect(n3_l[:]), ra[:], ACT.Copy)
             nc.scalar.activation(y[:].indirect(n4_l[:]), rb[:], ACT.Copy)
             nc.sync.dma_start(out_rows[:, t, :], y[:])
-            for h in range(2):
-                nc.vector.tensor_copy(y_grouped[:, halves[h], t], y[:, halves[h]])
+            for half in halves:
+                nc.vector.tensor_copy(y_grouped[:, half, t], y[:, half])
 
         fetch(0)
         for t in range(1, PACK):
@@ -309,12 +266,11 @@ def tile_picked_twpqpullbeod_none_po_kernel(
         y_codes = tile([P, S], U32, "y_codes")
         y_plane = tile([P, S], U8, "y_plane")
         words_out = out_1[0].rearrange("p n t -> p (n t)").bitcast(I32)
-        for h in range(2):
+        for half in halves:
             nc.vector.quantize_mx(
-                y_codes[:, halves[h]].bitcast(FP8X4), y_plane[:, halves[h]],
-                y_grouped[:, halves[h], :].rearrange("p w t -> p (w t)"),
+                y_codes[:, half].bitcast(FP8X4), y_plane[:, half], y_grouped[:, half, :].rearrange("p w t -> p (w t)")
             )
-            nc.sync.dma_start(words_out[:, halves[h]], y_codes[:, halves[h]].bitcast(I32))
-        for q in range(4):
+            nc.sync.dma_start(words_out[:, half], y_codes[:, half].bitcast(I32))
+        for q in range(QUADS):
             queue = nc.scalar if q % 2 else nc.sync
             queue.dma_start(out_2[0, 4 * q : 4 * q + 4, :].bitcast(I32), y_plane[32 * q : 32 * q + 4, :].bitcast(I32))

@@ -14,8 +14,10 @@ ACT = mybir.ActivationFunctionType
 
 P = 128
 PACK = 4
-QUADS = 4
-SCALE_ROWS = 16
+QUAD = 32
+QUADS = P // QUAD
+QUAD_ROWS = 4
+BLOCK = 8
 S = 512
 HALF = S // 2
 PER_COLUMN = 16
@@ -23,7 +25,7 @@ LINE = 4
 ALIGN = 64
 SIXTEENTH = 0.0625
 
-Z_SPANS = (slice(0, 128), slice(128, 384), slice(384, 512))
+HALVES = (slice(0, HALF), slice(HALF, S))
 
 FLOPS = 3 * 2 * 512 * 512 * 512
 
@@ -44,8 +46,11 @@ def tile_picked_twpqpullbeod_none_po_kernel(
         def bank(name, index):
             return psum.tile([P, S], F32, name=name, tag="bank%d" % index)
 
-        def entries(span):
-            return slice(span.start // PER_COLUMN, span.stop // PER_COLUMN)
+        def entries(half):
+            return slice(half.start // PER_COLUMN, half.stop // PER_COLUMN)
+
+        def quad_rows(q):
+            return slice(QUAD_ROWS * q, QUAD_ROWS * (q + 1)), slice(QUAD * q, QUAD * q + QUAD_ROWS)
 
         def load_list(src, name):
             held = lists.tile(list(src.shape), U16, name=name)
@@ -64,10 +69,11 @@ def tile_picked_twpqpullbeod_none_po_kernel(
 
         def load_plane(held, src, queue):
             for q in range(QUADS):
-                queue.dma_start(held[32 * q : 32 * q + 4, :].bitcast(I32), src[0, 4 * q : 4 * q + 4, :].bitcast(I32))
+                rows, partitions = quad_rows(q)
+                queue.dma_start(held[partitions, :].bitcast(I32), src[0, rows, :].bitcast(I32))
 
         def load_spread(held, src):
-            nc.sync.dma_start(held[0 : P : P // SCALE_ROWS, :].bitcast(I32), src[0].bitcast(I32))
+            nc.sync.dma_start(held[0:P:BLOCK, :].bitcast(I32), src[0].bitcast(I32))
 
         def load_row_values(src, name):
             held = tile([P, PACK], F32, name)
@@ -120,8 +126,8 @@ def tile_picked_twpqpullbeod_none_po_kernel(
             nc.vector.tensor_copy(picked[:, S:], x_bytes[:].indirect(x_list[:]))
             dealt = tile([P, S], U8, name + "_dealt")
             deal_bytes(nc.vector.tensor_copy, dealt[:], picked[:, :S])
-            for v in range(4):
-                nc.sync.dma_start(plane[v:P:32, :].bitcast(I32), dealt[8 * v : P : 32, :].bitcast(I32))
+            for v in range(QUAD_ROWS):
+                nc.sync.dma_start(plane[v:P:QUAD, :].bitcast(I32), dealt[BLOCK * v : P : QUAD, :].bitcast(I32))
             return picked[:, S:]
 
         def pick_words(table, which, name, tag):
@@ -162,15 +168,14 @@ def tile_picked_twpqpullbeod_none_po_kernel(
         deal_words(nc.vector.tensor_copy, d_k1_dealt, d_k1)
         a_banks = product(d_k1_dealt, a_plane, x_offs, a_x_plane, "a_acc", PACK)
 
-        halves = [slice(HALF * h, HALF * (h + 1)) for h in range(2)]
         b_far = []
         for t in range(PACK):
             b_rows = tile([P, S], F32, "b_rows%d" % t)
             nc.scalar.activation(b_rows[:], b_banks[t][:], ACT.Copy, scale=SIXTEENTH)
-            far = tile([P, S], F32, "b_far%d" % t)
-            for half in halves:
-                nc.scalar.activation(far[:, half], b_rows[:].indirect(n2_l[:, entries(half)]), ACT.Copy)
-            b_far.append(far)
+            fetched = tile([P, S], F32, "b_far%d" % t)
+            for half in HALVES:
+                nc.scalar.activation(fetched[:, half], b_rows[:].indirect(n2_l[:, entries(half)]), ACT.Copy)
+            b_far.append(fetched)
 
         b_diff = [tile([P, S], F32, "b_diff%d" % t) for t in range(PACK)]
         a_rows = [tile([P, S], F32, "a_rows%d" % t) for t in range(PACK)]
@@ -186,28 +191,27 @@ def tile_picked_twpqpullbeod_none_po_kernel(
             subtract_b(t)
 
         z_codes, z_planes = [], []
-        for index, span in enumerate(Z_SPANS):
-            width = span.stop - span.start
-            a_far = tile([P, PACK, width], F32, "a_far%d" % index)
-            stay = tile([P, PACK, width], F32, "stay%d" % index)
-            a_diff = tile([P, PACK, width], F32, "a_diff%d" % index)
-            back = tile([P, PACK, width], F32, "back%d" % index)
+        for index, half in enumerate(HALVES):
+            a_far = tile([P, PACK, HALF], F32, "a_far%d" % index)
+            stay = tile([P, PACK, HALF], F32, "stay%d" % index)
+            a_diff = tile([P, PACK, HALF], F32, "a_diff%d" % index)
+            back = tile([P, PACK, HALF], F32, "back%d" % index)
             for t in range(PACK):
-                nc.scalar.activation(a_far[:, t, :], a_rows[t][:].indirect(n1_l[:, entries(span)]), ACT.Copy)
-                nc.scalar.activation(stay[:, t, :], b_diff[t][:, span], ACT.Sigmoid, scale=-1.0)
+                nc.scalar.activation(a_far[:, t, :], a_rows[t][:].indirect(n1_l[:, entries(half)]), ACT.Copy)
+                nc.scalar.activation(stay[:, t, :], b_diff[t][:, half], ACT.Sigmoid, scale=-1.0)
                 nc.vector.scalar_tensor_tensor(
-                    a_diff[:, t, :], a_banks[t][:, span], gain_down[:, t : t + 1], a_far[:, t, :], ALU.mult, ALU.add
+                    a_diff[:, t, :], a_banks[t][:, half], gain_down[:, t : t + 1], a_far[:, t, :], ALU.mult, ALU.add
                 )
                 nc.vector.tensor_tensor(back[:, t, :], stay[:, t, :], a_diff[:, t, :], ALU.mult)
-            z_grouped = tile([P, width, PACK], BF16, "z_grouped%d" % index)
+            z_grouped = tile([P, HALF, PACK], BF16, "z_grouped%d" % index)
             nc.vector.tensor_tensor(
                 z_grouped[:].rearrange("p (c i) t -> p c t i", i=LINE),
                 a_far[:].rearrange("p t (c i) -> p c t i", i=LINE),
                 back[:].rearrange("p t (c i) -> p c t i", i=LINE),
                 ALU.subtract,
             )
-            codes = tile([P, width], U32, "z_codes%d" % index)
-            plane = tile([P, width], U8, "z_plane%d" % index)
+            codes = tile([P, HALF], U32, "z_codes%d" % index)
+            plane = tile([P, HALF], U8, "z_plane%d" % index)
             nc.vector.quantize_mx(codes[:].bitcast(FP8X4), plane[:], z_grouped[:].rearrange("p w t -> p (w t)"))
             z_codes.append(codes)
             z_planes.append(plane)
@@ -216,17 +220,17 @@ def tile_picked_twpqpullbeod_none_po_kernel(
         deal_words(nc.scalar.copy, w_dealt, w_raw)
         h_rows = [tile([P, S], F32, "h_rows%d" % t) for t in range(PACK)]
         h_banks = [bank("h_acc%d" % t, t) for t in range(PACK)]
-        for index, span in enumerate(Z_SPANS):
+        for index, half in enumerate(HALVES):
             for t in range(PACK):
                 cols = slice(P * t, P * (t + 1))
                 nc.tensor.matmul_mx(
-                    h_banks[t][:, span], lhsT=w_dealt[:, cols].bitcast(FP8X4), lhsT_scale=w_plane[:, cols],
+                    h_banks[t][:, half], lhsT=w_dealt[:, cols].bitcast(FP8X4), lhsT_scale=w_plane[:, cols],
                     rhs=z_codes[index][:].bitcast(FP8X4), rhs_scale=z_planes[index][:], start=True, stop=True,
                 )
-                if index < len(Z_SPANS) - 1 or t == 0:
-                    nc.scalar.activation(h_rows[t][:, span], h_banks[t][:, span], ACT.Copy)
+                if index == 0 or t == 0:
+                    nc.scalar.activation(h_rows[t][:, half], h_banks[t][:, half], ACT.Copy)
                 else:
-                    nc.vector.tensor_copy(h_rows[t][:, span], h_banks[t][:, span])
+                    nc.vector.tensor_copy(h_rows[t][:, half], h_banks[t][:, half])
 
         y_grouped = tile([P, S, PACK], BF16, "y_grouped")
         out_rows = out_0.rearrange("(p t) j -> p t j", t=PACK)
@@ -254,7 +258,7 @@ def tile_picked_twpqpullbeod_none_po_kernel(
             nc.scalar.activation(y[:].indirect(n3_l[:]), ra[:], ACT.Copy)
             nc.scalar.activation(y[:].indirect(n4_l[:]), rb[:], ACT.Copy)
             nc.sync.dma_start(out_rows[:, t, :], y[:])
-            for half in halves:
+            for half in HALVES:
                 nc.vector.tensor_copy(y_grouped[:, half, t], y[:, half])
 
         fetch(0)
@@ -266,11 +270,12 @@ def tile_picked_twpqpullbeod_none_po_kernel(
         y_codes = tile([P, S], U32, "y_codes")
         y_plane = tile([P, S], U8, "y_plane")
         words_out = out_1[0].rearrange("p n t -> p (n t)").bitcast(I32)
-        for half in halves:
+        for half in HALVES:
             nc.vector.quantize_mx(
                 y_codes[:, half].bitcast(FP8X4), y_plane[:, half], y_grouped[:, half, :].rearrange("p w t -> p (w t)")
             )
             nc.sync.dma_start(words_out[:, half], y_codes[:, half].bitcast(I32))
         for q in range(QUADS):
             queue = nc.scalar if q % 2 else nc.sync
-            queue.dma_start(out_2[0, 4 * q : 4 * q + 4, :].bitcast(I32), y_plane[32 * q : 32 * q + 4, :].bitcast(I32))
+            rows, partitions = quad_rows(q)
+            queue.dma_start(out_2[0, rows, :].bitcast(I32), y_plane[partitions, :].bitcast(I32))

from contextlib import ExitStack

import concourse.mybir as mybir

F32 = mybir.dt.float32
BF16 = mybir.dt.bfloat16
I32 = mybir.dt.int32
U32 = mybir.dt.uint32
U16 = mybir.dt.uint16
U8 = mybir.dt.uint8
FP8X4 = mybir.dt.float8_e4m3fn_x4
ALU = mybir.AluOpType
ACT = mybir.ActivationFunctionType

P = 128
PACK = 4
QUAD = 32
QUADS = P // QUAD
QUAD_ROWS = 4
BLOCK = 8
S = 512
HALF = S // 2
PER_COLUMN = 16
LINE = 4
ALIGN = 64
SIXTEENTH = 0.0625

HALVES = (slice(0, HALF), slice(HALF, S))

FLOPS = 3 * 2 * 512 * 512 * 512


def tile_picked_twpqpullbeod_none_po_kernel(
    tc, x_words, x_scales, d_words, d_scales, gn, w1_words, w1_scales, sl, th,
    offs, k1, two, k2, n1, n2, n3, n4, out_0, out_1, out_2,
):
    nc = tc.nc
    with ExitStack() as ctx:
        lists = ctx.enter_context(tc.tile_pool(name="lists", bufs=1))
        sbuf = ctx.enter_context(tc.tile_pool(name="sbuf", bufs=1))
        psum = ctx.enter_context(tc.psum_pool(name="psum", bufs=1))

        def tile(shape, dtype, name, tag=None):
            return sbuf.tile(shape, dtype, name=name, tag=tag or name, align_bytes=ALIGN)

        def bank(name, index):
            return psum.tile([P, S], F32, name=name, tag="bank%d" % index)

        def entries(half):
            return slice(half.start // PER_COLUMN, half.stop // PER_COLUMN)

        def quad_rows(q):
            return slice(QUAD_ROWS * q, QUAD_ROWS * (q + 1)), slice(QUAD * q, QUAD * q + QUAD_ROWS)

        def load_list(src, name):
            held = lists.tile(list(src.shape), U16, name=name)
            nc.sync.dma_start(held[:], src)
            return held

        def load_words(src, name):
            held = tile([P, src.shape[2]], U32, name)
            nc.sync.dma_start(held[:].bitcast(I32), src[0].rearrange("p n t -> p (n t)").bitcast(I32))
            return held

        def zeroed_bytes(width, name, engine):
            held = tile([P, width], U8, name)
            engine.memset(held[:].bitcast(I32), 0)
            return held

        def load_plane(held, src, queue):
            for q in range(QUADS):
                rows, partitions = quad_rows(q)
                queue.dma_start(held[partitions, :].bitcast(I32), src[0, rows, :].bitcast(I32))

        def load_spread(held, src):
            nc.sync.dma_start(held[0:P:BLOCK, :].bitcast(I32), src[0].bitcast(I32))

        def load_row_values(src, name):
            held = tile([P, PACK], F32, name)
            nc.gpsimd.dma_start(held[:], src.rearrange("(p t) o -> p (t o)", t=PACK))
            return held

        def deal_words(copy, dst, src):
            copy(
                dst[:].rearrange("p (t c i) -> p c t i", t=PACK, i=LINE),
                src[:].rearrange("p (c i t) -> p c t i", t=PACK, i=LINE),
            )

        def deal_bytes(copy, dst, src):
            copy(dst.rearrange("p (t m) -> p t m", t=PACK), src.rearrange("p (m t) -> p t m", t=PACK))

        two_l = load_list(two, "two_l")
        k2_l = load_list(k2, "k2_l")
        d_bytes = zeroed_bytes(d_scales.shape[2], "d_bytes", nc.gpsimd)
        load_spread(d_bytes, d_scales)
        x_bytes = zeroed_bytes(x_scales.shape[2], "x_bytes", nc.vector)
        load_plane(x_bytes, x_scales, nc.sync)
        x_table = load_words(x_words, "x_table")
        d_table = load_words(d_words, "d_table")
        k1_l = load_list(k1, "k1_l")
        offs_l = load_list(offs, "offs_l")
        w_raw = load_words(w1_words, "w_raw")

        gain = load_row_values(gn, "gain")
        warm = tile([P, 1], F32, "warm")
        nc.scalar.activation(warm[:], gain[:, 0:1], ACT.Sigmoid)
        slope = load_row_values(sl, "slope")
        thresh = load_row_values(th, "thresh")
        gain_up = tile([P, PACK], F32, "gain_up")
        gain_down = tile([P, PACK], F32, "gain_down")
        for scaled, factor in ((gain_up, SIXTEENTH), (gain_down, -SIXTEENTH)):
            nc.gpsimd.tensor_scalar(scaled[:], gain[:], factor, 0.0, ALU.mult, ALU.add)
        shift = tile([P, PACK], F32, "shift")
        nc.gpsimd.tensor_tensor(shift[:], slope[:], thresh[:], ALU.mult)
        bias = tile([P, PACK], F32, "bias")
        nc.gpsimd.tensor_scalar(bias[:], shift[:], -1.0, 0.0, ALU.mult, ALU.add)
        w_raw_bytes = zeroed_bytes(S, "w_raw_bytes", nc.gpsimd)
        load_plane(w_raw_bytes, w1_scales, nc.gpsimd)

        b_plane = zeroed_bytes(S, "b_plane", nc.vector)
        a_plane = zeroed_bytes(S, "a_plane", nc.vector)

        def pick_scales(d_list, x_list, plane, name, tag):
            picked = tile([P, 2 * S], U8, name + "_picked", tag)
            nc.vector.tensor_copy(picked[:, :S], d_bytes[:].indirect(d_list[:]))
            nc.vector.tensor_copy(picked[:, S:], x_bytes[:].indirect(x_list[:]))
            dealt = tile([P, S], U8, name + "_dealt")
            deal_bytes(nc.vector.tensor_copy, dealt[:], picked[:, :S])
            for v in range(QUAD_ROWS):
                nc.sync.dma_start(plane[v:P:QUAD, :].bitcast(I32), dealt[BLOCK * v : P : QUAD, :].bitcast(I32))
            return picked[:, S:]

        def pick_words(table, which, name, tag):
            picked = tile([P, S], U32, name, tag)
            nc.vector.tensor_copy(picked[:], table[:].indirect(which[:]))
            return picked

        def product(d_dealt, d_plane, x_picked, x_plane, name, first_bank):
            banks = []
            for t in range(PACK):
                acc = bank("%s%d" % (name, t), first_bank + t)
                cols = slice(P * t, P * (t + 1))
                nc.tensor.matmul_mx(
                    acc[:], lhsT=d_dealt[:, cols].bitcast(FP8X4), lhsT_scale=d_plane[:, cols],
                    rhs=x_picked[:].bitcast(FP8X4), rhs_scale=x_plane, start=True, stop=True,
                )
                banks.append(acc)
            return banks

        b_x_plane = pick_scales(k2_l, two_l, b_plane, "b_bytes", None)
        n2_l = load_list(n2, "n2_l")
        x_two = pick_words(x_table, two_l, "x_two", "x_picked")
        d_k2 = pick_words(d_table, k2_l, "d_k2", "d_picked")
        d_k2_dealt = tile([P, S], U32, "d_k2_dealt", "d_dealt")
        deal_words(nc.vector.tensor_copy, d_k2_dealt, d_k2)
        b_banks = product(d_k2_dealt, b_plane, x_two, b_x_plane, "b_acc", 0)

        w_plane = tile([P, S], U8, "w_plane")
        deal_bytes(nc.gpsimd.tensor_copy, w_plane[:], w_raw_bytes[:])

        a_x_plane = pick_scales(k1_l, offs_l, a_plane, "a_bytes", "d_picked")
        n1_l = load_list(n1, "n1_l")
        n3_l = load_list(n3, "n3_l")
        n4_l = load_list(n4, "n4_l")
        d_k1 = pick_words(d_table, k1_l, "d_k1", "d_dealt")
        x_offs = pick_words(x_table, offs_l, "x_offs", "x_picked")
        d_k1_dealt = tile([P, S], U32, "d_k1_dealt")
        deal_words(nc.vector.tensor_copy, d_k1_dealt, d_k1)
        a_banks = product(d_k1_dealt, a_plane, x_offs, a_x_plane, "a_acc", PACK)

        b_far = []
        for t in range(PACK):
            b_rows = tile([P, S], F32, "b_rows%d" % t)
            nc.scalar.activation(b_rows[:], b_banks[t][:], ACT.Copy, scale=SIXTEENTH)
            fetched = tile([P, S], F32, "b_far%d" % t)
            for half in HALVES:
                nc.scalar.activation(fetched[:, half], b_rows[:].indirect(n2_l[:, entries(half)]), ACT.Copy)
            b_far.append(fetched)

        b_diff = [tile([P, S], F32, "b_diff%d" % t) for t in range(PACK)]
        a_rows = [tile([P, S], F32, "a_rows%d" % t) for t in range(PACK)]

        def subtract_b(t):
            nc.vector.scalar_tensor_tensor(b_diff[t][:], b_banks[t][:], -SIXTEENTH, b_far[t][:], ALU.mult, ALU.add)

        for t in range(PACK // 2):
            subtract_b(t)
        for t in range(PACK):
            nc.vector.tensor_scalar(a_rows[t][:], a_banks[t][:], gain_up[:, t : t + 1], None, ALU.mult)
        for t in range(PACK // 2, PACK):
            subtract_b(t)

        z_codes, z_planes = [], []
        for index, half in enumerate(HALVES):
            a_far = tile([P, PACK, HALF], F32, "a_far%d" % index)
            stay = tile([P, PACK, HALF], F32, "stay%d" % index)
            a_diff = tile([P, PACK, HALF], F32, "a_diff%d" % index)
            back = tile([P, PACK, HALF], F32, "back%d" % index)
            for t in range(PACK):
                nc.scalar.activation(a_far[:, t, :], a_rows[t][:].indirect(n1_l[:, entries(half)]), ACT.Copy)
                nc.scalar.activation(stay[:, t, :], b_diff[t][:, half], ACT.Sigmoid, scale=-1.0)
                nc.vector.scalar_tensor_tensor(
                    a_diff[:, t, :], a_banks[t][:, half], gain_down[:, t : t + 1], a_far[:, t, :], ALU.mult, ALU.add
                )
                nc.vector.tensor_tensor(back[:, t, :], stay[:, t, :], a_diff[:, t, :], ALU.mult)
            z_grouped = tile([P, HALF, PACK], BF16, "z_grouped%d" % index)
            nc.vector.tensor_tensor(
                z_grouped[:].rearrange("p (c i) t -> p c t i", i=LINE),
                a_far[:].rearrange("p t (c i) -> p c t i", i=LINE),
                back[:].rearrange("p t (c i) -> p c t i", i=LINE),
                ALU.subtract,
            )
            codes = tile([P, HALF], U32, "z_codes%d" % index)
            plane = tile([P, HALF], U8, "z_plane%d" % index)
            nc.vector.quantize_mx(codes[:].bitcast(FP8X4), plane[:], z_grouped[:].rearrange("p w t -> p (w t)"))
            z_codes.append(codes)
            z_planes.append(plane)

        w_dealt = tile([P, S], U32, "w_dealt")
        deal_words(nc.scalar.copy, w_dealt, w_raw)
        h_rows = [tile([P, S], F32, "h_rows%d" % t) for t in range(PACK)]
        h_banks = [bank("h_acc%d" % t, t) for t in range(PACK)]
        for index, half in enumerate(HALVES):
            for t in range(PACK):
                cols = slice(P * t, P * (t + 1))
                nc.tensor.matmul_mx(
                    h_banks[t][:, half], lhsT=w_dealt[:, cols].bitcast(FP8X4), lhsT_scale=w_plane[:, cols],
                    rhs=z_codes[index][:].bitcast(FP8X4), rhs_scale=z_planes[index][:], start=True, stop=True,
                )
                if index == 0 or t == 0:
                    nc.scalar.activation(h_rows[t][:, half], h_banks[t][:, half], ACT.Copy)
                else:
                    nc.vector.tensor_copy(h_rows[t][:, half], h_banks[t][:, half])

        y_grouped = tile([P, S, PACK], BF16, "y_grouped")
        out_rows = out_0.rearrange("(p t) j -> p t j", t=PACK)
        results = []

        def fetch(t):
            rows, col = h_rows[t], slice(t, t + 1)
            sg2 = tile([P, HALF], F32, "sg2_%d" % t)
            pa = tile([P, HALF], F32, "pa%d" % t)
            sg = tile([P, HALF], F32, "sg_%d" % t)
            pb = tile([P, HALF], F32, "pb%d" % t)
            nc.scalar.activation(sg2[:], rows[:].indirect(n4_l[:]), ACT.Sigmoid, bias=bias[:, col], scale=slope[:, col])
            nc.scalar.activation(pa[:], rows[:].indirect(n3_l[:]), ACT.Copy)
            nc.scalar.activation(sg[:], rows[:].indirect(n3_l[:]), ACT.Sigmoid, bias=bias[:, col], scale=slope[:, col])
            nc.scalar.activation(pb[:], rows[:].indirect(n4_l[:]), ACT.Copy)
            ra = tile([P, HALF], F32, "ra%d" % t)
            rb = tile([P, HALF], F32, "rb%d" % t)
            nc.vector.tensor_tensor(ra[:], pa[:], sg2[:], ALU.mult)
            nc.vector.tensor_tensor(rb[:], pb[:], sg[:], ALU.subtract)
            results.append((ra, rb))

        def put(t):
            ra, rb = results[t]
            y = tile([P, S], F32, "y%d" % t)
            nc.scalar.activation(y[:].indirect(n3_l[:]), ra[:], ACT.Copy)
            nc.scalar.activation(y[:].indirect(n4_l[:]), rb[:], ACT.Copy)
            nc.sync.dma_start(out_rows[:, t, :], y[:])
            for half in HALVES:
                nc.vector.tensor_copy(y_grouped[:, half, t], y[:, half])

        fetch(0)
        for t in range(1, PACK):
            fetch(t)
            put(t - 1)
        put(PACK - 1)

        y_codes = tile([P, S], U32, "y_codes")
        y_plane = tile([P, S], U8, "y_plane")
        words_out = out_1[0].rearrange("p n t -> p (n t)").bitcast(I32)
        for half in HALVES:
            nc.vector.quantize_mx(
                y_codes[:, half].bitcast(FP8X4), y_plane[:, half], y_grouped[:, half, :].rearrange("p w t -> p (w t)")
            )
            nc.sync.dma_start(words_out[:, half], y_codes[:, half].bitcast(I32))
        for q in range(QUADS):
            queue = nc.scalar if q % 2 else nc.sync
            rows, partitions = quad_rows(q)
            queue.dma_start(out_2[0, rows, :].bitcast(I32), y_plane[partitions, :].bitcast(I32))
